import numpy as np
import ml_dtypes


def mxq(x, axis, fmt="e4m3"):
    dtype, down = {"e4m3": (ml_dtypes.float8_e4m3fn, 7), "e5m2": (ml_dtypes.float8_e5m2, 14)}[fmt]
    v = np.moveaxis(np.asarray(x, np.float32).astype(ml_dtypes.bfloat16).astype(np.float64), axis, -1)
    blocks = v.reshape(v.shape[:-1] + (-1, 32))
    amax = np.abs(blocks).max(-1, keepdims=True)
    byte = np.maximum(np.where(amax > 0, np.frexp(amax)[1] - 1 + 127, 0) - down, 1)
    scale = np.exp2(byte - 127.0)
    codes = (blocks / scale).astype(np.float32).astype(dtype).astype(np.float64)
    return np.moveaxis((codes * scale).reshape(v.shape), -1, axis)


WIDE = False


def mx_kscale(k, group=512):
    if not WIDE:
        return np.ones(k)
    levels = np.array([18, -18])
    if group != 512:
        return np.exp2(np.random.permutation(np.resize(levels, k // group))).repeat(group)
    if k % 512:
        return np.exp2(np.random.permutation(np.resize(levels, k // 32))).repeat(32)
    a = np.empty((k // 512, 16))
    for p in range(k // 512):
        a[p, :8] = np.random.permutation(np.resize(levels, 8))
        for g in range(8):
            far = levels[np.abs(levels - a[p, g]) >= 10]
            a[p, g + 8] = far[np.random.randint(len(far))]
    return np.exp2(a.ravel()).repeat(32)


def f64(x):
    return np.asarray(x).astype(np.float64)


def sigmoid(v):
    return 1.0 / (1.0 + np.exp(-v))


G, D, I, N, E, O = 4, 128, 128, 512, 128, 256


def sgn(shape):
    return np.random.uniform(0.5, 2.0, shape) * np.where(np.random.standard_normal(shape) < 0, -1.0, 1.0)


def setup_inputs():
    n = np.random.standard_normal
    s_d = mx_kscale(D, 0)
    s_i = mx_kscale(I, 0)
    s_ge = mx_kscale(G * E).reshape(G, E)
    return {
        "kT": (n((G, D, I)) / np.sqrt(D) / s_d[:, None]).astype(np.float32),
        "qT": (n((G, D, N)) * s_d[:, None]).astype(np.float32),
        "t": (sgn((G, I, 1)) * s_i[:, None]).astype(np.float32),
        "v": (n((G, I, E)) / np.sqrt(I) / s_i[:, None] * s_ge[:, None, :]).astype(np.float32),
        "wo": (n((G, E, O)) / np.sqrt(G * E) / s_ge[:, :, None]).astype(np.float32),
        "og": (n((O, N))).astype(np.float32),
    }


def reference(kT, qT, t, v, wo, og):
    kTq = mxq(f64(kT), 1, "e4m3")
    qTq = mxq(f64(qT), 1, "e4m3")
    z = kTq.transpose(0, 2, 1) @ qTq
    p = np.square(np.maximum(z, 0.0)) * f64(t)
    vq = mxq(f64(v), 1, "e4m3")
    pq = mxq(p, 1, "e4m3")
    y = vq.transpose(0, 2, 1) @ pq
    woq = mxq((f64(wo)).reshape(G * E, -1), 0, "e4m3")
    yq = mxq((y).reshape(G * E, -1), 0, "e4m3")
    u = woq.T @ yq
    out_ = u * sigmoid(f64(og))
    return out_

from contextlib import ExitStack

import concourse.mybir as mybir

G, D, I, N, E, O = 4, 128, 128, 512, 128, 256
FLOPS = 2 * G * D * I * N + 2 * G * I * E * N + 2 * G * E * O * N

F32 = mybir.dt.float32
BF16 = mybir.dt.bfloat16
U32 = mybir.dt.uint32
I32 = mybir.dt.int32
U8 = mybir.dt.uint8
FP8X4 = mybir.dt.float8_e4m3fn_x4
ALU = mybir.AluOpType
ACT = mybir.ActivationFunctionType

P = 128
R = 32
QUADS = P // R
PACK = 4
W = 128
OPERAND = W + W // PACK
ROTATION_RUNS = {1: [(0, 2), (2, 3), (3, 4)], 2: [(0, 2), (2, 4)], 3: [(2, 4), (1, 2), (0, 1)]}


def tile_rows_heads_relu2_gate_kernel(tc, kT, qT, t, v, wo, og, out):
    nc = tc.nc
    with ExitStack() as ctx:
        sb = ctx.enter_context(tc.tile_pool(name="sb", bufs=1))
        ps = ctx.enter_context(tc.psum_pool(name="ps", bufs=1))
        ctx.enter_context(tc.manual_schedule())

        def tiles(name, count, shape, dtype):
            return [sb.tile(shape, dtype, name="%s%d" % (name, x), align_bytes=64) for x in range(count)]

        k_raw = sb.tile([P, PACK, I], F32, name="k_raw")
        q_first = sb.tile([P, PACK, 2 * W], F32, name="q_first")
        q_rest = tiles("q_rest", 2, [P, PACK, W], F32)
        q_raw = [q_first[:, :, 0:W], q_first[:, :, W : 2 * W], q_rest[0][:], q_rest[1][:]]
        v_raw = sb.tile([P, PACK, E], F32, name="v_raw")
        wo_raw = sb.tile([P, PACK, O], F32, name="wo_raw")
        og_raw = sb.tile([P, 2, N], F32, name="og_raw")
        t_all = sb.tile([P, G, PACK], F32, name="t_all")
        t_own = sb.tile([P, PACK], F32, name="t_own")
        t_step = sb.tile([P, PACK], F32, name="t_step")
        t_sign = sb.tile([P, PACK], F32, name="t_sign")
        t_abs = sb.tile([P, G * PACK], F32, name="t_abs")
        root_cols = sb.tile([P, G * PACK, R], F32, name="root_cols", align_bytes=64)
        root = sb.tile([P, G, W], F32, name="root", align_bytes=64)
        zeros = sb.tile([P, 8], F32, name="zeros")
        warm_out = sb.tile([P, 8], F32, name="warm_out")

        k_bf = sb.tile([P, PACK * W], BF16, name="k_bf", align_bytes=64)
        q_bf = tiles("q_bf", QUADS, [P, PACK * W], BF16)
        v_bf = sb.tile([P, PACK * W], BF16, name="v_bf", align_bytes=64)
        wo_bf = sb.tile([P, PACK * O], BF16, name="wo_bf", align_bytes=64)
        k_mx = sb.tile([P, OPERAND], U32, name="k_mx", align_bytes=64)
        q_mx = tiles("q_mx", QUADS, [P, OPERAND], U32)
        v_mx = tiles("v_mx", QUADS, [P, OPERAND], U32)
        wo_mx = tiles("wo_mx", QUADS, [P, 2 * OPERAND], U32)
        scaled = tiles("scaled", G, [P, QUADS, W], F32)
        p_rows = tiles("p_rows", G, [P, PACK * W], BF16)
        p_turned = tiles("p_turned", G, [P, 2 * W], F32)
        p_bf = tiles("p_bf", G, [P, PACK * W], BF16)
        p_mx = tiles("p_mx", G, [P, OPERAND], U32)
        y_rows = tiles("y_rows", G, [P, PACK * W], BF16)
        y_turned = tiles("y_turned", G, [P, 2 * W], F32)
        y_bf = tiles("y_bf", G, [P, PACK * W], BF16)
        y_by_head = sb.tile([P, G, OPERAND], U32, name="y_by_head", align_bytes=64)
        y_by_block = sb.tile([P, QUADS, OPERAND], U32, name="y_by_block", align_bytes=64)
        gate = sb.tile([P, 2, N], F32, name="gate")
        result = tiles("result", 4, [P, 2 * W], F32)

        bank = [ps.tile([P, QUADS, W], F32, name="bank%d" % c) for c in range(QUADS)]
        u_bank = [ps.tile([P, 2, W], F32, name="u_bank%d" % x) for x in range(4)]

        def quad(c):
            return slice(R * c, R * (c + 1))

        def codes(operand):
            return operand[:, 0:W].bitcast(FP8X4)

        def scales(operand):
            return operand[:, W:OPERAND].bitcast(U8)

        def quantize(operand, src):
            nc.vector.quantize_mx(out=codes(operand), scales=scales(operand), in_=src)

        def product(dst, stationary, moving):
            nc.tensor.matmul_mx(out=dst, lhsT=codes(stationary), lhsT_scale=scales(stationary), rhs=codes(moving),
                                rhs_scale=scales(moving), start=True, stop=True)

        def interleave(copy, dst, raw):
            copy(out=dst.rearrange("p (c x j) -> p c j x", x=4, j=PACK), in_=raw.rearrange("p j (c x) -> p c j x", x=4))

        def rotate(rotations):
            for u, runs in ROTATION_RUNS.items():
                for first, end in runs:
                    to = (first + u) % QUADS
                    nc.sync.dma_start(out=rotations[u][R * to : R * (to + end - first), :].bitcast(I32),
                                      in_=rotations[0][R * first : R * end, :].bitcast(I32))

        def scores(g, a):
            product(bank[g][:, (a + g) % QUADS, :], q_mx[a][quad(g), :], k_mx[quad(g), :])

        def scale_scores(g, s):
            nc.vector.scalar_tensor_tensor(
                out=scaled[g][:, s : s + 2, :], in0=bank[g][:, s : s + 2, :], scalar=0.0,
                in1=root[:, g : g + 1, :].to_broadcast([P, 2, W]), op0=ALU.max, op1=ALU.mult)

        def square(g, s):
            nc.scalar.activation(
                out=p_rows[g][:, W * s : W * (s + 2)].rearrange("p (c m e) -> p c m e", m=R, e=2),
                in_=scaled[g][:, s : s + 2, :].rearrange("p s (h e m) -> p (s h) m e", h=2, e=2), func=ACT.Square)

        def turn(dst, rows):
            nc.vector.transpose(out=dst[:], in_=rows[:].bitcast(F32))

        def join_pairs(copy, dst, turned):
            copy(out=dst[:].bitcast(F32).rearrange("p (c r h) -> p c r h", c=QUADS, h=2),
                 in_=turned[:].rearrange("p (c h r) -> p c r h", c=QUADS, h=2))

        def values(g):
            for b in range(QUADS):
                product(bank[b][:, g, :], p_mx[g][quad(b), :], v_mx[(b - g) % QUADS][quad(b), :])

        def round_values(g):
            for b in range(QUADS):
                nc.scalar.copy(
                    out=y_rows[g][:, W * b : W * (b + 1)].rearrange("p (h m e) -> p h m e", h=2, e=2),
                    in_=bank[b][:, g, :].rearrange("p (m h e) -> p h m e", h=2, e=2))

        def quantize_y(g):
            quantize(y_by_head[:, G - 1 - g, :], y_bf[g][:])

        def y_move(g, s, count):
            a = (s - g) % QUADS
            return {"out": y_by_block[quad(s), a : a + count, :].bitcast(I32),
                    "in_": y_by_head[quad(s), G - 1 - g : G - 1 - g + count, :].bitcast(I32)}

        nc.gpsimd.memset(zeros[:], 0.0)
        nc.gpsimd.memset(v_mx[0][:, W:OPERAND], 0)
        nc.gpsimd.memset(wo_mx[0][:, O : 2 * OPERAND], 0)
        nc.gpsimd.memset(y_by_head[:, :, W:OPERAND], 0)

        q_view = qT.rearrange("g (p j) n -> (g p) j n", j=PACK)
        nc.sync.dma_start(out=q_first[:], in_=q_view[:, :, 0 : 2 * W])
        for c in range(QUADS):
            nc.sync.dma_start(out=t_all[quad(c), :, :], in_=t.rearrange("g (m j) o -> m g (j o)", j=PACK))
        nc.sync.dma_start(out=k_raw[:], in_=kT.rearrange("g (p j) i -> (g p) j i", j=PACK))
        nc.sync.dma_start(out=q_rest[0][:], in_=q_view[:, :, 2 * W : 3 * W])
        nc.sync.dma_start(out=t_own[:], in_=t.rearrange("g (m j) o -> (g m) (j o)", j=PACK))
        nc.sync.dma_start(out=q_rest[1][:], in_=q_view[:, :, 3 * W : 4 * W])
        nc.sync.dma_start(out=v_raw[:], in_=v.rearrange("g (p j) e -> (g p) j e", j=PACK))
        nc.sync.dma_start(out=wo_raw[:], in_=wo.rearrange("g (p j) o -> (g p) j o", j=PACK))
        nc.scalar.activation(out=warm_out[:], in_=zeros[:], func=ACT.Sqrt)

        interleave(nc.vector.tensor_copy, q_bf[0][:], q_raw[0])
        interleave(nc.vector.tensor_copy, q_bf[1][:], q_raw[1])
        quantize(q_mx[0], q_bf[0][:])
        nc.scalar.activation(out=t_abs[:], in_=t_all[:].rearrange("p g j -> p (g j)"), func=ACT.Abs)
        nc.scalar.activation(out=root_cols[:], in_=t_abs[:].unsqueeze(2).to_broadcast([P, G * PACK, R]), func=ACT.Sqrt)
        nc.vector.tensor_copy(out=k_bf[:].rearrange("p (x m j) -> p m j x", x=PACK, j=PACK),
                              in_=k_raw[:].rearrange("p j (m x) -> p m j x", x=PACK))
        quantize(q_mx[1], q_bf[1][:])
        quantize(k_mx, k_bf[:])
        nc.vector.transpose(out=root[:].rearrange("p g w -> p (g w)"), in_=root_cols[:].rearrange("p c r -> p (c r)"))
        interleave(nc.scalar.copy, q_bf[2][:], q_raw[2])
        nc.gpsimd.tensor_scalar(out=t_step[:], in0=t_own[:], scalar1=0.0, scalar2=2.0, op0=ALU.is_ge, op1=ALU.mult)
        nc.gpsimd.tensor_scalar(out=t_sign[:], in0=t_step[:], scalar1=1.0, scalar2=-1.0, op0=ALU.mult, op1=ALU.add)

        for g in range(G):
            scores(g, 0)
            scores(g, 1)
        quantize(q_mx[2], q_bf[2][:])
        interleave(nc.scalar.copy, q_bf[3][:], q_raw[3])
        scale_scores(0, 0)
        for g in (1, 2, 3, 0):
            scores(g, 2)
        square(0, 0)
        nc.vector.tensor_tensor(out=v_bf[:].rearrange("p (w j) -> p w j", j=PACK), in0=v_raw[:].rearrange("p j w -> p w j"),
                                in1=t_sign[:].unsqueeze(1).to_broadcast([P, E, PACK]), op=ALU.mult)
        quantize(q_mx[3], q_bf[3][:])
        scale_scores(1, 2)
        for g in (0, 1, 2):
            scores(g, 3)
        square(1, 2)
        quantize(v_mx[0], v_bf[:])
        rotate(v_mx)
        nc.sync.dma_start(out=og_raw[:], in_=og.rearrange("(h p) n -> p h n", p=P))
        for h in (1, 0):
            nc.gpsimd.tensor_scalar(
                out=wo_bf[:, PACK * W * h : PACK * W * (h + 1)].rearrange("p (w j) -> p w j", j=PACK),
                in0=wo_raw[:, :, W * h : W * (h + 1)].rearrange("p j w -> p w j"),
                scalar1=1.0, scalar2=0.0, op0=ALU.mult, op1=ALU.add)
        scale_scores(3, 0)
        scores(3, 3)
        for g, s in ((0, 2), (1, 0), (2, 2), (2, 0)):
            scale_scores(g, s)
            square(g, s)

        turn(p_turned[0], p_rows[0])
        join_pairs(nc.scalar.copy, p_bf[0], p_turned[0])
        turn(p_turned[1], p_rows[1])
        square(3, 0)
        join_pairs(nc.scalar.copy, p_bf[1], p_turned[1])
        scale_scores(3, 2)
        square(3, 2)
        quantize(p_mx[0], p_bf[0][:])
        values(0)
        turn(p_turned[2], p_rows[2])
        quantize(p_mx[1], p_bf[1][:])
        round_values(0)
        values(1)
        join_pairs(nc.vector.tensor_copy, p_bf[2], p_turned[2])
        turn(p_turned[3], p_rows[3])
        quantize(p_mx[2], p_bf[2][:])
        round_values(1)
        values(2)
        join_pairs(nc.vector.tensor_copy, p_bf[3], p_turned[3])
        nc.vector.quantize_mx(out=wo_mx[0][:, 0:O].bitcast(FP8X4), scales=wo_mx[0][:, O : 2 * OPERAND].bitcast(U8),
                              in_=wo_bf[:])
        rotate(wo_mx)
        turn(y_turned[0], y_rows[0])
        quantize(p_mx[3], p_bf[3][:])
        round_values(2)
        values(3)
        join_pairs(nc.vector.tensor_copy, y_bf[0], y_turned[0])
        turn(y_turned[1], y_rows[1])
        quantize_y(0)
        join_pairs(nc.vector.tensor_copy, y_bf[1], y_turned[1])
        turn(y_turned[2], y_rows[2])
        quantize_y(1)
        for g, s, count in ((0, 0, 1), (1, 0, 1), (1, 1, 2), (1, 2, 2), (1, 3, 2)):
            nc.sync.dma_start(**y_move(g, s, count))
        round_values(3)
        for h in range(2):
            nc.scalar.activation(out=gate[:, h, :], in_=og_raw[:, h, :], func=ACT.Sigmoid)
        turn(y_turned[3], y_rows[3])
        join_pairs(nc.vector.tensor_copy, y_bf[2], y_turned[2])
        join_pairs(nc.vector.tensor_copy, y_bf[3], y_turned[3])
        quantize_y(2)
        quantize_y(3)
        for g, s, count in ((2, 2, 1), (3, 3, 2), (3, 0, 2), (3, 1, 2), (3, 2, 1)):
            nc.vector.tensor_copy(**y_move(g, s, count))

        pieces = [(2 * half + h, h, 2 * half) for half in range(2) for h in range(2)]
        for x, h, first in pieces:
            for a in (first, first + 1):
                nc.tensor.matmul_mx(
                    out=u_bank[x][:, a - first, :], lhsT=wo_mx[a][:, W * h : W * (h + 1)].bitcast(FP8X4),
                    lhsT_scale=wo_mx[a][:, O : 2 * OPERAND].bitcast(U8)[:, W * h : W * (h + 1)],
                    rhs=codes(y_by_block[:, a, :]), rhs_scale=scales(y_by_block[:, a, :]), start=True, stop=True)
        out_view = out.rearrange("(h p) n -> p h n", p=P)
        for x, h, first in pieces:
            cols = slice(W * first, W * (first + 2))
            nc.vector.tensor_tensor(out=result[x][:], in0=u_bank[x][:].rearrange("p a w -> p (a w)"),
                                    in1=gate[:, h, cols], op=ALU.mult)
            nc.sync.dma_start(out=out_view[:, h, cols], in_=result[x][:])
